import numpy as np
import ml_dtypes


def mxq(x, axis, fmt="e4m3"):
    dtype, down = {"e4m3": (ml_dtypes.float8_e4m3fn, 7), "e5m2": (ml_dtypes.float8_e5m2, 14)}[fmt]
    v = np.moveaxis(np.asarray(x, np.float32).astype(ml_dtypes.bfloat16).astype(np.float64), axis, -1)
    blocks = v.reshape(v.shape[:-1] + (-1, 32))
    amax = np.abs(blocks).max(-1, keepdims=True)
    byte = np.maximum(np.where(amax > 0, np.frexp(amax)[1] - 1 + 127, 0) - down, 1)
    scale = np.exp2(byte - 127.0)
    codes = (blocks / scale).astype(np.float32).astype(dtype).astype(np.float64)
    return np.moveaxis((codes * scale).reshape(v.shape), -1, axis)


WIDE = False


def mx_kscale(k):
    if not WIDE:
        return np.ones(k)
    levels = np.array([10, -10, 5, -5, 0])
    if k % 512:
        return np.exp2(np.random.permutation(np.resize(levels, k // 32))).repeat(32)
    a = np.empty((k // 512, 16))
    for p in range(k // 512):
        a[p, :8] = np.random.permutation(np.resize(levels, 8))
        for g in range(8):
            far = levels[np.abs(levels - a[p, g]) >= 10]
            a[p, g + 8] = far[np.random.randint(len(far))]
    return np.exp2(a.ravel()).repeat(32)


def f64(x):
    return np.asarray(x).astype(np.float64)


def striped(idx):
    return np.tile(np.asarray(idx).reshape(-1, 16).T, (8, 1)).astype(np.uint16)


def unstriped(offs):
    return offs[:16].T.reshape(-1).astype(np.int64)


E2M1 = np.array([0.0, 0.5, 1.0, 1.5, 2.0, 3.0, 4.0, 6.0, -0.0, -0.5, -1.0, -1.5, -2.0, -3.0, -4.0, -6.0])


def pack_weight(w, fmt):
    k, n = w.shape
    w = f64(np.asarray(w, np.float32).astype(ml_dtypes.bfloat16)).reshape(k // 32, 32, n)
    amax = np.abs(w).max(1)
    if fmt == "e4m3":
        byte = np.frexp(amax)[1] - 1 + 127 - 7
    else:
        mant, ex = np.frexp(amax / 6.0)
        byte = np.where(mant > 0.5, ex, ex - 1) + 127
    byte = np.clip(np.where(amax > 0, byte, 1), 1, 254)
    scaled = (w * np.exp2(127.0 - byte)[:, None, :]).reshape(k, n).astype(np.float32)
    by_word = np.ascontiguousarray(scaled.reshape(k // 512, 128, 4, n).transpose(0, 1, 3, 2))
    if fmt == "e4m3":
        words = by_word.astype(ml_dtypes.float8_e4m3fn).view(np.uint8)
    else:
        c = by_word.astype(ml_dtypes.float4_e2m1fn).view(np.uint8) & 0xF
        words = (c[..., 0::2] | (c[..., 1::2] << 4)).reshape(k // 512, 128, 2 * n)
    return np.ascontiguousarray(words), np.ascontiguousarray(byte.astype(np.uint8).reshape(k // 512, 16, n))


def unpack_weight(words, scales, fmt):
    g, _, n = scales.shape
    words = np.ascontiguousarray(words).reshape(g, 128, n, -1)
    if fmt == "e4m3":
        vals = words.view(ml_dtypes.float8_e4m3fn).astype(np.float64)
    else:
        nib = np.empty((g, 128, n, 4), np.uint8)
        nib[..., 0::2] = words & 0xF
        nib[..., 1::2] = words >> 4
        vals = E2M1[nib]
    vals = vals * np.repeat(np.exp2(scales.astype(np.float64) - 127.0), 8, axis=1)[..., None]
    return vals.transpose(0, 1, 3, 2).reshape(g * 512, n)


D, E, T, I, Q = 512, 512, 2048, 512, 128


def setup_inputs():
    n = np.random.standard_normal
    idx = np.random.permutation(T)[:I]
    fd = mx_kscale(D)
    fe = mx_kscale(E)
    keysp = pack_weight(n((D, T)) / fd[:, None], "e2m1")
    valsp = pack_weight(n((E, T)) / fe[:, None], "e2m1")
    return {
        "query": (n((D, Q)) * 1.0 / np.sqrt(D) * fd[:, None]).astype(np.float32),
        "keys_words": keysp[0],
        "keys_scales": keysp[1],
        "aim": (np.random.uniform(0.5, 2.0, (Q, 1))).astype(np.float32),
        "soft": (np.random.uniform(0.5, 2.0, (Q, 1))).astype(np.float32),
        "gout": (n((E, Q)) * 1 / np.sqrt(E) * fe[:, None]).astype(np.float32),
        "vals_words": valsp[0],
        "vals_scales": valsp[1],
        "base": (0.5 * n((Q, I))).astype(np.float32),
        "offs": striped(idx),
    }


def reference(query, keys_words, keys_scales, aim, soft, gout, vals_words, vals_scales, base, offs):
    idx = unstriped(offs)
    keysu = unpack_weight(keys_words, keys_scales, "e2m1")
    valsu = unpack_weight(vals_words, vals_scales, "e2m1")
    queryq = mxq(f64(query), 0, "e4m3")
    keysidxg = keysu[:, idx]
    a = queryq.T @ keysidxg
    p = 1.0 / (np.square(f64(aim) - a) + f64(soft))
    z = np.sum(p, axis=1, keepdims=True)
    goutq = mxq(f64(gout), 0, "e4m3")
    valsidxg = valsu[:, idx]
    c0 = goutq.T @ valsidxg
    dz = np.sum(c0 * p / np.square(z) * (-1.0), axis=1, keepdims=True)
    dp = c0 / z + dz
    da = dp * (-1.0) / np.square(np.square(f64(aim) - a) + f64(soft)) * (f64(aim) - a) * 2.0 * (-1.0)
    hda = da * 512.0 * 2.0 * 512.0
    hdp = hda * (-1.0) * 2.0 * (f64(aim) - a) / np.square(np.square(f64(aim) - a) + f64(soft)) * (-1.0)
    hdz = np.sum(hdp, axis=1, keepdims=True)
    hz = np.sum(hdp * c0 / np.square(z) * (-1.0), axis=1, keepdims=True) + np.sum(hdz * (-1.0) * c0 * p / np.square(np.square(z)) * (-1.0), axis=1, keepdims=True) * z * 2.0
    hp = hdz * (-1.0) / np.square(z) * c0 + hz
    ha = hda * (-1.0) * 2.0 * (f64(aim) - a) * dp * (-1.0) / np.square(np.square(np.square(f64(aim) - a) + f64(soft))) * (-1.0) * (np.square(f64(aim) - a) + f64(soft)) * 2.0 * (f64(aim) - a) * 2.0 * (-1.0) - hda * (-1.0) * 2.0 * dp * (-1.0) / np.square(np.square(f64(aim) - a) + f64(soft)) - hp * (-1.0) / np.square(np.square(f64(aim) - a) + f64(soft)) * (f64(aim) - a) * 2.0
    y = ha + f64(base)
    return y

@@ -1,0 +1,158 @@
+from contextlib import ExitStack
+
+import concourse.mybir as mybir
+
+F32 = mybir.dt.float32
+BF16 = mybir.dt.bfloat16
+I32 = mybir.dt.int32
+U32 = mybir.dt.uint32
+U16 = mybir.dt.uint16
+U8 = mybir.dt.uint8
+FP8X4 = mybir.dt.float8_e4m3fn_x4
+FP4X4 = mybir.dt.float4_e2m1fn_x4
+ACT = mybir.ActivationFunctionType
+ADD = mybir.AluOpType.add
+SUB = mybir.AluOpType.subtract
+MULT = mybir.AluOpType.mult
+
+P = 128
+PACK = 4
+T = 2048
+I = 512
+Q = 128
+FLOPS = 2 * 2 * 512 * Q * I
+
+
+def tile_attend_gpnearpoint_kernel(tc, query, keys_words, keys_scales, aim, soft, gout, vals_words, vals_scales, base, offs, out):
+    nc = tc.nc
+    with ExitStack() as ctx:
+        sb = ctx.enter_context(tc.tile_pool(name="sb", bufs=1))
+        ps = ctx.enter_context(tc.psum_pool(name="ps", bufs=1))
+
+        def tile(name, shape, dtype=F32):
+            return sb.tile(shape, dtype, name=name, align_bytes=64)
+
+        offsets = tile("offsets", [P, I // 16], U16)
+        ks = tile("ks", [P, T], U8)
+        vs = sb.tile([P, T], U8, name="vs", tag="vs", align_bytes=64)
+        kw = sb.tile([P, T], U16, name="kw", tag="kw", align_bytes=64)
+        q_raw = tile("q_raw", [P, PACK, Q])
+        g_raw = sb.tile([P, PACK, Q], F32, name="g_raw", tag="g_raw", align_bytes=64)
+        aim_c = tile("aim_c", [P, 1])
+        soft_c = tile("soft_c", [P, 1])
+        six = tile("six", [P, 1])
+        warm = sb.tile([P, 1], F32, name="warm", tag="vw", align_bytes=64)
+
+        nc.vector.memset(ks[:].bitcast(I32), 0)
+        nc.vector.memset(six[:], 6.0)
+        nc.vector.memset(vs[:].bitcast(I32), 0)
+
+        def load_scales(queue, dst, src, quads):
+            for quad in quads:
+                queue.dma_start(dst[32 * quad : 32 * quad + 4, :].bitcast(I32), src[0, 4 * quad : 4 * quad + 4, :].bitcast(I32))
+
+        nc.scalar.activation(warm[:], six[:], ACT.Abs_reciprocal_sqrt)
+        vw = sb.tile([P, T], U16, name="vw", tag="vw", align_bytes=64)
+
+        nc.sync.dma_start(offsets[:], offs)
+        nc.sync.dma_start(kw[:].bitcast(I32), keys_words[0].bitcast(I32))
+        nc.sync.dma_start(q_raw[:], query.rearrange("(p j) q -> p j q", j=PACK))
+        load_scales(nc.sync, ks, keys_scales, range(4))
+        nc.sync.dma_start(g_raw[:], gout.rearrange("(p j) q -> p j q", j=PACK))
+        nc.gpsimd.dma_start(aim_c[:], aim)
+        load_scales(nc.gpsimd, vs, vals_scales, [3])
+        nc.gpsimd.dma_start(soft_c[:], soft)
+        load_scales(nc.sync, vs, vals_scales, range(3))
+        nc.sync.dma_start(vw[:].bitcast(I32), vals_words[0].bitcast(I32))
+
+        def interleave(name, raw):
+            grouped = tile(name, [P, Q, PACK], BF16)
+            nc.scalar.copy(grouped[:], raw[:].rearrange("p j q -> p q j"))
+            return grouped
+
+        def quantize(name, grouped):
+            codes = tile(name + "_codes", [P, Q], U32)
+            scales = tile(name + "_scales", [P, Q], U8)
+            nc.vector.quantize_mx(out=codes[:].bitcast(FP8X4), scales=scales[:], in_=grouped[:].rearrange("p q j -> p (q j)"))
+            return codes, scales
+
+        def gather(picked, window, cols):
+            nc.vector.tensor_copy(picked[:, cols], window[:].indirect(offsets[:, cols.start // 16 : cols.stop // 16]))
+
+        def product(bank, codes, scales, words, word_scales):
+            nc.tensor.matmul_mx(out=bank, lhsT=codes[:].bitcast(FP8X4), lhsT_scale=scales[:], rhs=words.bitcast(FP4X4), rhs_scale=word_scales, start=True, stop=True)
+
+        whole = slice(0, I)
+        halves = [slice(0, I // 2), slice(I // 2, I)]
+        ksg = tile("ksg", [P, I], U8)
+        vsg = tile("vsg", [P, I], U8)
+        kwg = tile("kwg", [P, I], U16)
+        vwg = tile("vwg", [P, I], U16)
+        a = [ps.tile([Q, I // 2], F32, name="a%d" % h) for h in range(2)]
+        c = ps.tile([Q, I], F32, name="c")
+
+        q_bf = interleave("q_bf", q_raw)
+        g_bf = interleave("g_bf", g_raw)
+        gather(kwg, kw, whole)
+        base_t = sb.tile([P, I], F32, name="base_t", tag="kw", align_bytes=64)
+        nc.sync.dma_start(base_t[:], base)
+        q_codes, q_scales = quantize("q", q_bf)
+        for h, cols in enumerate(halves):
+            gather(ksg, ks, cols)
+            product(a[h][:], q_codes, q_scales, kwg[:, cols], ksg[:, cols])
+        gather(vsg, vs, whole)
+        g_codes, g_scales = quantize("g", g_bf)
+        gather(vwg, vw, whole)
+        product(c[:], g_codes, g_scales, vwg[:], vsg[:])
+
+        usq = sb.tile([P, I], F32, name="usq", tag="g_raw", align_bytes=64)
+        dsq = tile("dsq", [P, I])
+        p = tile("p", [P, I])
+        p2 = tile("p2", [P, I])
+        z = tile("z", [P, 1])
+        for h, cols in enumerate(halves):
+            nc.scalar.activation(usq[:, cols], a[h][:], ACT.Square, bias=aim_c[:], scale=-1.0)
+        for cols in halves:
+            nc.scalar.activation(dsq[:, cols], usq[:, cols], ACT.Square, bias=soft_c[:])
+        nc.scalar.activation(p[:], dsq[:], ACT.Abs_reciprocal_sqrt, accum_out=z[:])
+        nc.scalar.activation(p2[:], p[:], ACT.Square)
+
+        late = sb.tile([P, 2 * I + 8], F32, name="late", tag="vw", align_bytes=64)
+        x = late[:, 0:I]
+        w = late[:, I : 2 * I]
+        rz = late[:, 2 * I : 2 * I + 1]
+        nkap = tile("nkap", [P, 1])
+        bcoef = tile("bcoef", [P, 1])
+        nc.vector.reciprocal(rz, z[:])
+        nc.gpsimd.tensor_scalar(nkap[:], rz, rz, -4194304.0, MULT, MULT)
+        nc.gpsimd.tensor_scalar(bcoef[:], nkap[:], rz, -1.0, MULT, MULT)
+
+        qq = tile("qq", [P, I])
+        junk = tile("junk", [P, I])
+        junk2 = tile("junk2", [P, I])
+        junk3 = tile("junk3", [P, I])
+        t = tile("t", [P, I])
+        r1 = tile("r1", [P, I])
+        r2 = tile("r2", [P, I])
+        r3 = tile("r3", [P, I])
+        res = tile("res", [P, I])
+        m = tile("m", [P, 1])
+        alpha = tile("alpha", [P, 1])
+        bsum = tile("bsum", [P, 1])
+        beta = tile("beta", [P, 1])
+        nc.vector.scalar_tensor_tensor(x, usq[:], 2.0, p[:], MULT, MULT)
+        for h, cols in enumerate(halves):
+            nc.vector.scalar_tensor_tensor(w[:, cols], a[h][:], aim_c[:], p2[:, cols], SUB, MULT)
+        nc.vector.scalar_tensor_tensor(junk[:], c[:], rz, p[:], MULT, MULT, accum_out=m[:])
+        nc.vector.scalar_tensor_tensor(qq[:], x, 0.5, p2[:], SUB, MULT)
+        nc.vector.scalar_tensor_tensor(t[:], c[:], m[:], w, SUB, MULT)
+        nc.scalar.activation(junk2[:], t[:], ACT.Square, accum_out=bsum[:])
+        nc.scalar.activation(beta[:], bsum[:], ACT.Copy, scale=bcoef[:])
+        nc.vector.scalar_tensor_tensor(r1[:], c[:], m[:], qq[:], SUB, MULT)
+        nc.vector.scalar_tensor_tensor(junk3[:], t[:], rz, w, MULT, MULT, accum_out=alpha[:])
+        nc.vector.scalar_tensor_tensor(r3[:], w, beta[:], base_t[:], MULT, ADD)
+        for cols in halves:
+            nc.vector.scalar_tensor_tensor(r2[:, cols], r1[:, cols], alpha[:], t[:, cols], SUB, MULT)
+        for cols in halves:
+            nc.vector.scalar_tensor_tensor(res[:, cols], r2[:, cols], nkap[:], r3[:, cols], MULT, ADD)
+            nc.sync.dma_start(out[:, cols], res[:, cols])

@@ -44,7 +44,7 @@ def tile_attend_gpnearpoint_kernel(tc, query, keys_words, keys_scales, aim, soft
         warm = sb.tile([P, 1], F32, name="warm", tag="vw", align_bytes=64)
 
         nc.vector.memset(ks[:].bitcast(I32), 0)
-        nc.vector.memset(six[:], 6.0)
+        nc.vector.memset(six[:], 1.5)
         nc.vector.memset(vs[:].bitcast(I32), 0)
 
         def load_scales(queue, dst, src, quads):
@@ -60,10 +60,10 @@ def tile_attend_gpnearpoint_kernel(tc, query, keys_words, keys_scales, aim, soft
         load_scales(nc.sync, ks, keys_scales, range(4))
         nc.sync.dma_start(g_raw[:], gout.rearrange("(p j) q -> p j q", j=PACK))
         nc.gpsimd.dma_start(aim_c[:], aim)
-        load_scales(nc.gpsimd, vs, vals_scales, [3])
         nc.gpsimd.dma_start(soft_c[:], soft)
-        load_scales(nc.sync, vs, vals_scales, range(3))
+        load_scales(nc.sync, vs, vals_scales, [0])
         nc.sync.dma_start(vw[:].bitcast(I32), vals_words[0].bitcast(I32))
+        load_scales(nc.sync, vs, vals_scales, [1, 2, 3])
 
         def interleave(name, raw):
             grouped = tile(name, [P, Q, PACK], BF16)
@@ -100,9 +100,9 @@ def tile_attend_gpnearpoint_kernel(tc, query, keys_words, keys_scales, aim, soft
         for h, cols in enumerate(halves):
             gather(ksg, ks, cols)
             product(a[h][:], q_codes, q_scales, kwg[:, cols], ksg[:, cols])
-        gather(vsg, vs, whole)
-        g_codes, g_scales = quantize("g", g_bf)
         gather(vwg, vw, whole)
+        g_codes, g_scales = quantize("g", g_bf)
+        gather(vsg, vs, whole)
         product(c[:], g_codes, g_scales, vwg[:], vsg[:])
 
         usq = sb.tile([P, I], F32, name="usq", tag="g_raw", align_bytes=64)
@@ -110,17 +110,21 @@ def tile_attend_gpnearpoint_kernel(tc, query, keys_words, keys_scales, aim, soft
         p = tile("p", [P, I])
         p2 = tile("p2", [P, I])
         z = tile("z", [P, 1])
+        d4 = tile("d4", [P, I])
+        n = tile("n", [P, I])
+        s2 = tile("s2", [P, 1])
+        nc.gpsimd.tensor_scalar(s2[:], soft_c[:], -2.0, 0.0, MULT, ADD)
         for h, cols in enumerate(halves):
             nc.scalar.activation(usq[:, cols], a[h][:], ACT.Square, bias=aim_c[:], scale=-1.0)
-        for cols in halves:
             nc.scalar.activation(dsq[:, cols], usq[:, cols], ACT.Square, bias=soft_c[:])
+            nc.scalar.activation(d4[:, cols], dsq[:, cols], ACT.Square)
+        nc.scalar.activation(p2[:], d4[:], ACT.Abs_reciprocal_sqrt)
         nc.scalar.activation(p[:], dsq[:], ACT.Abs_reciprocal_sqrt, accum_out=z[:])
-        nc.scalar.activation(p2[:], p[:], ACT.Square)
+        nc.scalar.activation(n[:], p[:], ACT.Identity, bias=six[:], scale=s2[:])
 
-        late = sb.tile([P, 2 * I + 8], F32, name="late", tag="vw", align_bytes=64)
-        x = late[:, 0:I]
-        w = late[:, I : 2 * I]
-        rz = late[:, 2 * I : 2 * I + 1]
+        late = sb.tile([P, I + 8], F32, name="late", tag="vs", align_bytes=64)
+        w = late[:, 0:I]
+        rz = late[:, I : I + 1]
         nkap = tile("nkap", [P, 1])
         bcoef = tile("bcoef", [P, 1])
         nc.vector.reciprocal(rz, z[:])
@@ -140,11 +144,10 @@ def tile_attend_gpnearpoint_kernel(tc, query, keys_words, keys_scales, aim, soft
         alpha = tile("alpha", [P, 1])
         bsum = tile("bsum", [P, 1])
         beta = tile("beta", [P, 1])
-        nc.vector.scalar_tensor_tensor(x, usq[:], 2.0, p[:], MULT, MULT)
         for h, cols in enumerate(halves):
             nc.vector.scalar_tensor_tensor(w[:, cols], a[h][:], aim_c[:], p2[:, cols], SUB, MULT)
         nc.vector.scalar_tensor_tensor(junk[:], c[:], rz, p[:], MULT, MULT, accum_out=m[:])
-        nc.vector.scalar_tensor_tensor(qq[:], x, 0.5, p2[:], SUB, MULT)
+        nc.vector.tensor_tensor(qq[:], n[:], p2[:], MULT)
         nc.vector.scalar_tensor_tensor(t[:], c[:], m[:], w, SUB, MULT)
         nc.scalar.activation(junk2[:], t[:], ACT.Square, accum_out=bsum[:])
         nc.scalar.activation(beta[:], bsum[:], ACT.Copy, scale=bcoef[:])

from contextlib import ExitStack

import concourse.mybir as mybir

F32 = mybir.dt.float32
BF16 = mybir.dt.bfloat16
I32 = mybir.dt.int32
U32 = mybir.dt.uint32
U16 = mybir.dt.uint16
U8 = mybir.dt.uint8
FP8X4 = mybir.dt.float8_e4m3fn_x4
FP4X4 = mybir.dt.float4_e2m1fn_x4
ACT = mybir.ActivationFunctionType
ADD = mybir.AluOpType.add
SUB = mybir.AluOpType.subtract
MULT = mybir.AluOpType.mult

P = 128
PACK = 4
T = 2048
I = 512
Q = 128
FLOPS = 2 * 2 * 512 * Q * I


def tile_attend_gpnearpoint_kernel(tc, query, keys_words, keys_scales, aim, soft, gout, vals_words, vals_scales, base, offs, out):
    nc = tc.nc
    with ExitStack() as ctx:
        sb = ctx.enter_context(tc.tile_pool(name="sb", bufs=1))
        ps = ctx.enter_context(tc.psum_pool(name="ps", bufs=1))

        def tile(name, shape, dtype=F32):
            return sb.tile(shape, dtype, name=name, align_bytes=64)

        offsets = tile("offsets", [P, I // 16], U16)
        ks = tile("ks", [P, T], U8)
        vs = sb.tile([P, T], U8, name="vs", tag="vs", align_bytes=64)
        kw = sb.tile([P, T], U16, name="kw", tag="kw", align_bytes=64)
        q_raw = tile("q_raw", [P, PACK, Q])
        g_raw = sb.tile([P, PACK, Q], F32, name="g_raw", tag="g_raw", align_bytes=64)
        aim_c = tile("aim_c", [P, 1])
        soft_c = tile("soft_c", [P, 1])
        six = tile("six", [P, 1])
        warm = sb.tile([P, 1], F32, name="warm", tag="vw", align_bytes=64)

        nc.vector.memset(ks[:].bitcast(I32), 0)
        nc.vector.memset(six[:], 1.5)
        nc.vector.memset(vs[:].bitcast(I32), 0)

        def load_scales(queue, dst, src, quads):
            for quad in quads:
                queue.dma_start(dst[32 * quad : 32 * quad + 4, :].bitcast(I32), src[0, 4 * quad : 4 * quad + 4, :].bitcast(I32))

        nc.scalar.activation(warm[:], six[:], ACT.Abs_reciprocal_sqrt)
        vw = sb.tile([P, T], U16, name="vw", tag="vw", align_bytes=64)

        nc.sync.dma_start(offsets[:], offs)
        nc.sync.dma_start(kw[:].bitcast(I32), keys_words[0].bitcast(I32))
        nc.sync.dma_start(q_raw[:], query.rearrange("(p j) q -> p j q", j=PACK))
        load_scales(nc.sync, ks, keys_scales, range(4))
        nc.sync.dma_start(g_raw[:], gout.rearrange("(p j) q -> p j q", j=PACK))
        nc.gpsimd.dma_start(aim_c[:], aim)
        nc.gpsimd.dma_start(soft_c[:], soft)
        load_scales(nc.sync, vs, vals_scales, [0])
        nc.sync.dma_start(vw[:].bitcast(I32), vals_words[0].bitcast(I32))
        load_scales(nc.sync, vs, vals_scales, [1, 2, 3])

        def interleave(name, raw):
            grouped = tile(name, [P, Q, PACK], BF16)
            nc.scalar.copy(grouped[:], raw[:].rearrange("p j q -> p q j"))
            return grouped

        def quantize(name, grouped):
            codes = tile(name + "_codes", [P, Q], U32)
            scales = tile(name + "_scales", [P, Q], U8)
            nc.vector.quantize_mx(out=codes[:].bitcast(FP8X4), scales=scales[:], in_=grouped[:].rearrange("p q j -> p (q j)"))
            return codes, scales

        def gather(picked, window, cols):
            nc.vector.tensor_copy(picked[:, cols], window[:].indirect(offsets[:, cols.start // 16 : cols.stop // 16]))

        def product(bank, codes, scales, words, word_scales):
            nc.tensor.matmul_mx(out=bank, lhsT=codes[:].bitcast(FP8X4), lhsT_scale=scales[:], rhs=words.bitcast(FP4X4), rhs_scale=word_scales, start=True, stop=True)

        whole = slice(0, I)
        halves = [slice(0, I // 2), slice(I // 2, I)]
        ksg = tile("ksg", [P, I], U8)
        vsg = tile("vsg", [P, I], U8)
        kwg = tile("kwg", [P, I], U16)
        vwg = tile("vwg", [P, I], U16)
        a = [ps.tile([Q, I // 2], F32, name="a%d" % h) for h in range(2)]
        c = ps.tile([Q, I], F32, name="c")

        q_bf = interleave("q_bf", q_raw)
        g_bf = interleave("g_bf", g_raw)
        gather(kwg, kw, whole)
        base_t = sb.tile([P, I], F32, name="base_t", tag="kw", align_bytes=64)
        nc.sync.dma_start(base_t[:], base)
        q_codes, q_scales = quantize("q", q_bf)
        for h, cols in enumerate(halves):
            gather(ksg, ks, cols)
            product(a[h][:], q_codes, q_scales, kwg[:, cols], ksg[:, cols])
        gather(vwg, vw, whole)
        g_codes, g_scales = quantize("g", g_bf)
        gather(vsg, vs, whole)
        product(c[:], g_codes, g_scales, vwg[:], vsg[:])

        usq = sb.tile([P, I], F32, name="usq", tag="g_raw", align_bytes=64)
        dsq = tile("dsq", [P, I])
        p = tile("p", [P, I])
        p2 = tile("p2", [P, I])
        z = tile("z", [P, 1])
        d4 = tile("d4", [P, I])
        n = tile("n", [P, I])
        s2 = tile("s2", [P, 1])
        nc.gpsimd.tensor_scalar(s2[:], soft_c[:], -2.0, 0.0, MULT, ADD)
        for h, cols in enumerate(halves):
            nc.scalar.activation(usq[:, cols], a[h][:], ACT.Square, bias=aim_c[:], scale=-1.0)
            nc.scalar.activation(dsq[:, cols], usq[:, cols], ACT.Square, bias=soft_c[:])
            nc.scalar.activation(d4[:, cols], dsq[:, cols], ACT.Square)
        nc.scalar.activation(p2[:], d4[:], ACT.Abs_reciprocal_sqrt)
        nc.scalar.activation(p[:], dsq[:], ACT.Abs_reciprocal_sqrt, accum_out=z[:])
        nc.scalar.activation(n[:], p[:], ACT.Identity, bias=six[:], scale=s2[:])

        late = sb.tile([P, I + 8], F32, name="late", tag="vs", align_bytes=64)
        w = late[:, 0:I]
        rz = late[:, I : I + 1]
        nkap = tile("nkap", [P, 1])
        bcoef = tile("bcoef", [P, 1])
        nc.vector.reciprocal(rz, z[:])
        nc.gpsimd.tensor_scalar(nkap[:], rz, rz, -4194304.0, MULT, MULT)
        nc.gpsimd.tensor_scalar(bcoef[:], nkap[:], rz, -1.0, MULT, MULT)

        qq = tile("qq", [P, I])
        junk = tile("junk", [P, I])
        junk2 = tile("junk2", [P, I])
        junk3 = tile("junk3", [P, I])
        t = tile("t", [P, I])
        r1 = tile("r1", [P, I])
        r2 = tile("r2", [P, I])
        r3 = tile("r3", [P, I])
        res = tile("res", [P, I])
        m = tile("m", [P, 1])
        alpha = tile("alpha", [P, 1])
        bsum = tile("bsum", [P, 1])
        beta = tile("beta", [P, 1])
        for h, cols in enumerate(halves):
            nc.vector.scalar_tensor_tensor(w[:, cols], a[h][:], aim_c[:], p2[:, cols], SUB, MULT)
        nc.vector.scalar_tensor_tensor(junk[:], c[:], rz, p[:], MULT, MULT, accum_out=m[:])
        nc.vector.tensor_tensor(qq[:], n[:], p2[:], MULT)
        nc.vector.scalar_tensor_tensor(t[:], c[:], m[:], w, SUB, MULT)
        nc.scalar.activation(junk2[:], t[:], ACT.Square, accum_out=bsum[:])
        nc.scalar.activation(beta[:], bsum[:], ACT.Copy, scale=bcoef[:])
        nc.vector.scalar_tensor_tensor(r1[:], c[:], m[:], qq[:], SUB, MULT)
        nc.vector.scalar_tensor_tensor(junk3[:], t[:], rz, w, MULT, MULT, accum_out=alpha[:])
        nc.vector.scalar_tensor_tensor(r3[:], w, beta[:], base_t[:], MULT, ADD)
        for cols in halves:
            nc.vector.scalar_tensor_tensor(r2[:, cols], r1[:, cols], alpha[:], t[:, cols], SUB, MULT)
        for cols in halves:
            nc.vector.scalar_tensor_tensor(res[:, cols], r2[:, cols], nkap[:], r3[:, cols], MULT, ADD)
            nc.sync.dma_start(out[:, cols], res[:, cols])
